import numpy as np
import ml_dtypes


def mxq(x, axis, fmt="e4m3"):
    dtype, down = {"e4m3": (ml_dtypes.float8_e4m3fn, 7), "e5m2": (ml_dtypes.float8_e5m2, 14)}[fmt]
    v = np.moveaxis(np.asarray(x, np.float32).astype(ml_dtypes.bfloat16).astype(np.float64), axis, -1)
    blocks = v.reshape(v.shape[:-1] + (-1, 32))
    amax = np.abs(blocks).max(-1, keepdims=True)
    byte = np.maximum(np.where(amax > 0, np.frexp(amax)[1] - 1 + 127, 0) - down, 1)
    scale = np.exp2(byte - 127.0)
    codes = (blocks / scale).astype(np.float32).astype(dtype).astype(np.float64)
    return np.moveaxis((codes * scale).reshape(v.shape), -1, axis)


WIDE = False


def mx_kscale(k):
    if not WIDE:
        return np.ones(k)
    levels = np.array([10, -10, 5, -5, 0])
    if k % 512:
        return np.exp2(np.random.permutation(np.resize(levels, k // 32))).repeat(32)
    a = np.empty((k // 512, 16))
    for p in range(k // 512):
        a[p, :8] = np.random.permutation(np.resize(levels, 8))
        for g in range(8):
            far = levels[np.abs(levels - a[p, g]) >= 10]
            a[p, g + 8] = far[np.random.randint(len(far))]
    return np.exp2(a.ravel()).repeat(32)


def f64(x):
    return np.asarray(x).astype(np.float64)


def striped8(idx):
    return np.asarray(idx).reshape(8, -1, 16).transpose(0, 2, 1).reshape(128, -1).astype(np.uint16)


def unstriped8(offs):
    return offs.reshape(8, 16, -1).transpose(0, 2, 1).reshape(8, -1).astype(np.int64)


def pick8(x, idx, run):
    r = np.arange(len(x))
    return x[r[:, None], idx[r % (8 * run) // run]]


E2M1 = np.array([0.0, 0.5, 1.0, 1.5, 2.0, 3.0, 4.0, 6.0, -0.0, -0.5, -1.0, -1.5, -2.0, -3.0, -4.0, -6.0])


def pack_weight(w, fmt):
    k, n = w.shape
    w = f64(np.asarray(w, np.float32).astype(ml_dtypes.bfloat16)).reshape(k // 32, 32, n)
    amax = np.abs(w).max(1)
    if fmt == "e4m3":
        byte = np.frexp(amax)[1] - 1 + 127 - 7
    else:
        mant, ex = np.frexp(amax / 6.0)
        byte = np.where(mant > 0.5, ex, ex - 1) + 127
    byte = np.clip(np.where(amax > 0, byte, 1), 1, 254)
    scaled = (w * np.exp2(127.0 - byte)[:, None, :]).reshape(k, n).astype(np.float32)
    by_word = np.ascontiguousarray(scaled.reshape(k // 512, 128, 4, n).transpose(0, 1, 3, 2))
    if fmt == "e4m3":
        words = by_word.astype(ml_dtypes.float8_e4m3fn).view(np.uint8)
    else:
        c = by_word.astype(ml_dtypes.float4_e2m1fn).view(np.uint8) & 0xF
        words = (c[..., 0::2] | (c[..., 1::2] << 4)).reshape(k // 512, 128, 2 * n)
    return np.ascontiguousarray(words), np.ascontiguousarray(byte.astype(np.uint8).reshape(k // 512, 16, n))


def unpack_weight(words, scales, fmt):
    g, _, n = scales.shape
    words = np.ascontiguousarray(words).reshape(g, 128, n, -1)
    if fmt == "e4m3":
        vals = words.view(ml_dtypes.float8_e4m3fn).astype(np.float64)
    else:
        nib = np.empty((g, 128, n, 4), np.uint8)
        nib[..., 0::2] = words & 0xF
        nib[..., 1::2] = words >> 4
        vals = E2M1[nib]
    vals = vals * np.repeat(np.exp2(scales.astype(np.float64) - 127.0), 8, axis=1)[..., None]
    return vals.transpose(0, 1, 3, 2).reshape(g * 512, n)


D, T, U, I, Q = 512, 1024, 1024, 512, 128


def setup_inputs():
    n = np.random.standard_normal
    idx = np.stack([np.random.permutation(T)[:I] for _ in range(8)])
    idx2 = np.stack([np.random.permutation(U)[:I] for _ in range(8)])
    idx3 = np.stack([np.random.permutation(U)[:I] for _ in range(8)])
    idx4 = np.stack([np.random.permutation(U)[:I] for _ in range(8)])
    idx5 = np.stack([np.random.permutation(T)[:I] for _ in range(8)])
    idx6 = np.stack([np.random.permutation(T)[:I] for _ in range(8)])
    fd = mx_kscale(D)
    cachep = pack_weight(n((D, T)) / fd[:, None], "e4m3")
    draftp = pack_weight(n((D, U)) / fd[:, None], "e2m1")
    return {
        "query": (n((D, Q)) * 1.0 / np.sqrt(D) * fd[:, None]).astype(np.float32),
        "cache_words": cachep[0],
        "cache_scales": cachep[1],
        "draft_words": draftp[0],
        "draft_scales": draftp[1],
        "offs": striped8(idx),
        "offs2": striped8(idx2),
        "offs3": striped8(idx3),
        "offs4": striped8(idx4),
        "offs5": striped8(idx5),
        "offs6": striped8(idx6),
    }


def reference(query, cache_words, cache_scales, draft_words, draft_scales, offs, offs2, offs3, offs4, offs5, offs6):
    idx = unstriped8(offs)
    idx2 = unstriped8(offs2)
    idx3 = unstriped8(offs3)
    idx4 = unstriped8(offs4)
    idx5 = unstriped8(offs5)
    idx6 = unstriped8(offs6)
    cacheu = unpack_weight(cache_words, cache_scales, "e4m3")
    draftu = unpack_weight(draft_words, draft_scales, "e2m1")
    queryq = mxq(f64(query), 0, "e4m3")
    a = queryq.T @ cacheu
    b = queryq.T @ draftu
    f1 = np.zeros((Q, U))
    f1[np.arange(Q)[:, None], idx2[np.arange(Q) % 128 // 16]] = pick8(a, idx, 16)
    bb = b + f1
    w = np.maximum(pick8(bb, idx3, 16), pick8(bb, idx4, 16))
    f2 = np.zeros((Q, T))
    f2[np.arange(Q)[:, None], idx5[np.arange(Q) % 128 // 16]] = w
    aa = a - f2
    y = pick8(aa, idx6, 16)
    return y

@@ -1,0 +1,140 @@
+from contextlib import ExitStack
+
+import concourse.mybir as mybir
+
+D, T, U, I, Q = 512, 1024, 1024, 512, 128
+FLOPS = 2 * D * Q * (T + U)
+
+F32 = mybir.dt.float32
+BF16 = mybir.dt.bfloat16
+I32 = mybir.dt.int32
+U32 = mybir.dt.uint32
+U16 = mybir.dt.uint16
+U8 = mybir.dt.uint8
+FP8X4 = mybir.dt.float8_e4m3fn_x4
+FP4X4 = mybir.dt.float4_e2m1fn_x4
+COPY = mybir.ActivationFunctionType.Copy
+ALU = mybir.AluOpType
+
+P = 128
+PACK = 4
+BANK = 512
+HALF = I // 2
+A_PIECES = ((0, 512), (512, 768), (768, 896), (896, 1024))
+
+
+def tile_attend_doubleread_two_kernel(tc, query, cache_words, cache_scales, draft_words, draft_scales,
+                                       offs, offs2, offs3, offs4, offs5, offs6, out):
+    nc = tc.nc
+    with ExitStack() as ctx:
+        lists = ctx.enter_context(tc.tile_pool(name="lists", bufs=1))
+        sb = ctx.enter_context(tc.tile_pool(name="sb", bufs=1))
+        psum = ctx.enter_context(tc.psum_pool(name="psum", bufs=1))
+
+        def load_list(src, name):
+            tile = lists.tile([P, I // 16], U16, name=name)
+            nc.sync.dma_start(tile[:], src)
+            return tile
+
+        def half_of(tile, h):
+            return tile[:, h * (HALF // 16):(h + 1) * (HALF // 16)]
+
+        def load_scale_rows(plane, scales, queues):
+            for quad in range(4):
+                queues[quad].dma_start(plane[32 * quad:32 * quad + 4, :].bitcast(I32),
+                                       scales[0, 4 * quad:4 * quad + 4, :].bitcast(I32))
+
+        cache_plane = sb.tile([P, T], U8, name="cache_plane", align_bytes=64)
+        draft_plane = sb.tile([P, U], U8, name="draft_plane", align_bytes=64)
+        f1 = sb.tile([P, U], F32, name="f1")
+        f2 = sb.tile([P, T], F32, name="f2")
+        nc.vector.memset(cache_plane[:].bitcast(I32), 0)
+        nc.vector.memset(draft_plane[:].bitcast(I32), 0)
+        nc.vector.memset(f1[:], 0.0)
+        nc.vector.memset(f2[:], 0.0)
+
+        q_raw = sb.tile([P, PACK, Q], F32, name="q_raw")
+        nc.sync.dma_start(q_raw[:], query.rearrange("(p j) q -> p j q", j=PACK))
+        load_scale_rows(cache_plane, cache_scales, (nc.scalar, nc.sync, nc.scalar, nc.sync))
+        cache_bytes = cache_words[0].rearrange("p n t -> p (n t)")
+        cache_codes = []
+        for h in range(2):
+            codes = sb.tile([P, BANK], U32, name="cache_codes%d" % h, align_bytes=64)
+            nc.sync.dma_start(codes[:].bitcast(I32),
+                              cache_bytes[:, h * BANK * PACK:(h + 1) * BANK * PACK].bitcast(I32))
+            cache_codes.append(codes)
+        l1 = load_list(offs, "l1")
+        l2 = load_list(offs2, "l2")
+        draft_codes = sb.tile([P, 2 * U], U8, name="draft_codes", align_bytes=64)
+        nc.sync.dma_start(draft_codes[:].bitcast(I32), draft_words[0].bitcast(I32))
+        load_scale_rows(draft_plane, draft_scales, (nc.sync,) * 4)
+        l3 = load_list(offs3, "l3")
+        l4 = load_list(offs4, "l4")
+        l5 = load_list(offs5, "l5")
+        l6 = load_list(offs6, "l6")
+
+        q_bf = sb.tile([P, Q, PACK], BF16, name="q_bf", align_bytes=64)
+        q_view = q_raw[:].rearrange("p j q -> p q j")
+        nc.scalar.activation(q_bf[:, 0:Q // 2, :], q_view[:, 0:Q // 2, :], COPY)
+        nc.vector.tensor_copy(q_bf[:, Q // 2:Q, :], q_view[:, Q // 2:Q, :])
+        q_codes = sb.tile([P, Q], U32, name="q_codes", align_bytes=64)
+        q_plane = sb.tile([P, Q], U8, name="q_plane", align_bytes=64)
+        nc.vector.quantize_mx(q_codes[:].bitcast(FP8X4), q_plane[:], q_bf[:].rearrange("p q j -> p (q j)"))
+
+        a_sb = sb.tile([P, T], F32, name="a_sb")
+        a_banks = []
+        for n, (c0, c1) in enumerate(A_PIECES):
+            bank = psum.tile([P, BANK], F32, name="a_bank%d" % n)
+            h = c0 // BANK
+            nc.tensor.matmul_mx(bank[:, 0:c1 - c0], lhsT=q_codes[:].bitcast(FP8X4), lhsT_scale=q_plane[:],
+                                rhs=cache_codes[h][:, c0 - h * BANK:c1 - h * BANK].bitcast(FP8X4),
+                                rhs_scale=cache_plane[:, c0:c1], start=True, stop=True)
+            a_banks.append(bank)
+        for n, (c0, c1) in enumerate(A_PIECES):
+            if n in (0, 3):
+                nc.scalar.copy(a_sb[:, c0:c1], a_banks[n][:, 0:c1 - c0])
+            else:
+                nc.vector.tensor_copy(a_sb[:, c0:c1], a_banks[n][:, 0:c1 - c0])
+
+        b_banks = []
+        for h in range(2):
+            bank = psum.tile([P, BANK], F32, name="b_bank%d" % h)
+            nc.tensor.matmul_mx(bank[:], lhsT=q_codes[:].bitcast(FP8X4), lhsT_scale=q_plane[:],
+                                rhs=draft_codes[:, 2 * h * BANK:2 * (h + 1) * BANK].bitcast(FP4X4),
+                                rhs_scale=draft_plane[:, h * BANK:(h + 1) * BANK], start=True, stop=True)
+            b_banks.append(bank)
+
+        picked = sb.tile([P, I], F32, name="picked")
+        nc.scalar.activation(picked[:, 0:HALF], a_sb[:].indirect(half_of(l1, 0)), COPY)
+        nc.vector.tensor_copy(picked[:, HALF:I], a_sb[:].indirect(half_of(l1, 1)))
+        nc.scalar.activation(f1[:].indirect(l2[:]), picked[:], COPY)
+
+        bb = sb.tile([P, U], F32, name="bb")
+        for h in range(2):
+            cols = slice(h * BANK, (h + 1) * BANK)
+            nc.vector.tensor_tensor(bb[:, cols], b_banks[h][:], f1[:, cols], ALU.add)
+
+        for h in range(2):
+            g3 = sb.tile([P, HALF], F32, name="g3")
+            g4 = sb.tile([P, HALF], F32, name="g4")
+            w = sb.tile([P, HALF], F32, name="w%d" % h)
+            nc.vector.tensor_copy(g3[:], bb[:].indirect(half_of(l3, h)))
+            if h == 0:
+                nc.scalar.activation(g4[:], bb[:].indirect(half_of(l4, h)), COPY)
+            else:
+                nc.vector.tensor_copy(g4[:], bb[:].indirect(half_of(l4, h)))
+            nc.vector.tensor_tensor(w[:], g3[:], g4[:], ALU.max)
+            nc.scalar.activation(f2[:].indirect(half_of(l5, h)), w[:], COPY)
+
+        aa = sb.tile([P, T], F32, name="aa")
+        for n, (c0, c1) in enumerate(A_PIECES[:2]):
+            nc.vector.tensor_tensor(aa[:, c0:c1], a_banks[n][:, 0:c1 - c0], f2[:, c0:c1], ALU.subtract)
+        c0 = A_PIECES[2][0]
+        nc.vector.tensor_tensor(aa[:, c0:T], a_sb[:, c0:T], f2[:, c0:T], ALU.subtract)
+
+        y0 = sb.tile([P, HALF], F32, name="y0")
+        y1 = sb.tile([P, HALF], F32, name="y1")
+        nc.vector.tensor_copy(y0[:], aa[:].indirect(half_of(l6, 0)))
+        nc.scalar.activation(y1[:], aa[:].indirect(half_of(l6, 1)), COPY)
+        nc.sync.dma_start(out[:, 0:HALF], y0[:])
+        nc.scalar.dma_start(out[:, HALF:I], y1[:])

@@ -20,6 +20,7 @@ P = 128
 PACK = 4
 BANK = 512
 HALF = I // 2
+SPLIT = 704
 A_PIECES = ((0, 512), (512, 768), (768, 896), (896, 1024))
 
 
@@ -48,8 +49,6 @@ def tile_attend_doubleread_two_kernel(tc, query, cache_words, cache_scales, draf
         draft_plane = sb.tile([P, U], U8, name="draft_plane", align_bytes=64)
         f1 = sb.tile([P, U], F32, name="f1")
         f2 = sb.tile([P, T], F32, name="f2")
-        nc.vector.memset(cache_plane[:].bitcast(I32), 0)
-        nc.vector.memset(draft_plane[:].bitcast(I32), 0)
         nc.vector.memset(f1[:], 0.0)
         nc.vector.memset(f2[:], 0.0)
 
@@ -109,28 +108,29 @@ def tile_attend_doubleread_two_kernel(tc, query, cache_words, cache_scales, draf
         nc.vector.tensor_copy(picked[:, HALF:I], a_sb[:].indirect(half_of(l1, 1)))
         nc.scalar.activation(f1[:].indirect(l2[:]), picked[:], COPY)
 
+        b_tail = sb.tile([P, U - SPLIT], F32, name="b_tail")
+        nc.vector.tensor_copy(b_tail[:], b_banks[1][:, SPLIT - BANK:BANK])
         bb = sb.tile([P, U], F32, name="bb")
-        for h in range(2):
-            cols = slice(h * BANK, (h + 1) * BANK)
-            nc.vector.tensor_tensor(bb[:, cols], b_banks[h][:], f1[:, cols], ALU.add)
+        nc.vector.tensor_tensor(bb[:, 0:BANK], b_banks[0][:], f1[:, 0:BANK], ALU.add)
+        nc.vector.tensor_tensor(bb[:, BANK:SPLIT], b_banks[1][:, 0:SPLIT - BANK], f1[:, BANK:SPLIT], ALU.add)
+        nc.gpsimd.tensor_tensor(bb[:, SPLIT:U], b_tail[:], f1[:, SPLIT:U], ALU.add)
 
+        g4 = []
+        for h in range(2):
+            g = sb.tile([P, HALF], F32, name="g4_%d" % h)
+            nc.scalar.activation(g[:], bb[:].indirect(half_of(l4, h)), COPY)
+            g4.append(g)
         for h in range(2):
             g3 = sb.tile([P, HALF], F32, name="g3")
-            g4 = sb.tile([P, HALF], F32, name="g4")
             w = sb.tile([P, HALF], F32, name="w%d" % h)
             nc.vector.tensor_copy(g3[:], bb[:].indirect(half_of(l3, h)))
-            if h == 0:
-                nc.scalar.activation(g4[:], bb[:].indirect(half_of(l4, h)), COPY)
-            else:
-                nc.vector.tensor_copy(g4[:], bb[:].indirect(half_of(l4, h)))
-            nc.vector.tensor_tensor(w[:], g3[:], g4[:], ALU.max)
+            nc.vector.tensor_tensor(w[:], g3[:], g4[h][:], ALU.max)
             nc.scalar.activation(f2[:].indirect(half_of(l5, h)), w[:], COPY)
 
         aa = sb.tile([P, T], F32, name="aa")
-        for n, (c0, c1) in enumerate(A_PIECES[:2]):
-            nc.vector.tensor_tensor(aa[:, c0:c1], a_banks[n][:, 0:c1 - c0], f2[:, c0:c1], ALU.subtract)
-        c0 = A_PIECES[2][0]
-        nc.vector.tensor_tensor(aa[:, c0:T], a_sb[:, c0:T], f2[:, c0:T], ALU.subtract)
+        nc.vector.tensor_tensor(aa[:, 0:BANK], a_banks[0][:], f2[:, 0:BANK], ALU.subtract)
+        nc.vector.tensor_tensor(aa[:, BANK:SPLIT], a_banks[1][:, 0:SPLIT - BANK], f2[:, BANK:SPLIT], ALU.subtract)
+        nc.gpsimd.tensor_tensor(aa[:, SPLIT:T], a_sb[:, SPLIT:T], f2[:, SPLIT:T], ALU.subtract)
 
         y0 = sb.tile([P, HALF], F32, name="y0")
         y1 = sb.tile([P, HALF], F32, name="y1")

@@ -21,7 +21,8 @@ PACK = 4
 BANK = 512
 HALF = I // 2
 SPLIT = 704
-A_PIECES = ((0, 512), (512, 768), (768, 896), (896, 1024))
+CHUNK = T // 4
+A_PIECES = ((0, 256), (256, 512), (512, 768), (768, 896), (896, 1024))
 
 
 def tile_attend_doubleread_two_kernel(tc, query, cache_words, cache_scales, draft_words, draft_scales,
@@ -45,7 +46,7 @@ def tile_attend_doubleread_two_kernel(tc, query, cache_words, cache_scales, draf
                 queues[quad].dma_start(plane[32 * quad:32 * quad + 4, :].bitcast(I32),
                                        scales[0, 4 * quad:4 * quad + 4, :].bitcast(I32))
 
-        cache_plane = sb.tile([P, T], U8, name="cache_plane", align_bytes=64)
+        cache_plane = sb.tile([P, CHUNK], U8, name="cache_plane", align_bytes=64)
         draft_plane = sb.tile([P, U], U8, name="draft_plane", align_bytes=64)
         f1 = sb.tile([P, U], F32, name="f1")
         f2 = sb.tile([P, T], F32, name="f2")
@@ -54,7 +55,10 @@ def tile_attend_doubleread_two_kernel(tc, query, cache_words, cache_scales, draf
 
         q_raw = sb.tile([P, PACK, Q], F32, name="q_raw")
         nc.sync.dma_start(q_raw[:], query.rearrange("(p j) q -> p j q", j=PACK))
-        load_scale_rows(cache_plane, cache_scales, (nc.scalar, nc.sync, nc.scalar, nc.sync))
+        for quad, queue in enumerate((nc.scalar, nc.sync, nc.scalar, nc.sync)):
+            rows = cache_scales[0, 4 * quad:4 * quad + 4, :].bitcast(I32)
+            queue.dma_start(cache_plane[32 * quad:32 * quad + 16, :].bitcast(I32),
+                            rows.rearrange("r (j c) -> j r c", j=4))
         cache_bytes = cache_words[0].rearrange("p n t -> p (n t)")
         cache_codes = []
         for h in range(2):
@@ -83,21 +87,21 @@ def tile_attend_doubleread_two_kernel(tc, query, cache_words, cache_scales, draf
         a_sb = sb.tile([P, T], F32, name="a_sb")
         a_banks = []
         for n, (c0, c1) in enumerate(A_PIECES):
-            bank = psum.tile([P, BANK], F32, name="a_bank%d" % n)
+            bank = psum.tile([P, BANK], F32, name="a_bank%d" % n, tag="bank%d" % n)
             h = c0 // BANK
             nc.tensor.matmul_mx(bank[:, 0:c1 - c0], lhsT=q_codes[:].bitcast(FP8X4), lhsT_scale=q_plane[:],
                                 rhs=cache_codes[h][:, c0 - h * BANK:c1 - h * BANK].bitcast(FP8X4),
-                                rhs_scale=cache_plane[:, c0:c1], start=True, stop=True)
+                                rhs_scale=cache_plane[4 * (c0 // CHUNK):P, c0 % CHUNK:c0 % CHUNK + c1 - c0], start=True, stop=True)
             a_banks.append(bank)
         for n, (c0, c1) in enumerate(A_PIECES):
-            if n in (0, 3):
+            if n % 2 == 0:
                 nc.scalar.copy(a_sb[:, c0:c1], a_banks[n][:, 0:c1 - c0])
             else:
                 nc.vector.tensor_copy(a_sb[:, c0:c1], a_banks[n][:, 0:c1 - c0])
 
         b_banks = []
         for h in range(2):
-            bank = psum.tile([P, BANK], F32, name="b_bank%d" % h)
+            bank = psum.tile([P, BANK], F32, name="b_bank%d" % h, tag="bank%d" % (3 + h))
             nc.tensor.matmul_mx(bank[:], lhsT=q_codes[:].bitcast(FP8X4), lhsT_scale=q_plane[:],
                                 rhs=draft_codes[:, 2 * h * BANK:2 * (h + 1) * BANK].bitcast(FP4X4),
                                 rhs_scale=draft_plane[:, h * BANK:(h + 1) * BANK], start=True, stop=True)
@@ -108,12 +112,13 @@ def tile_attend_doubleread_two_kernel(tc, query, cache_words, cache_scales, draf
         nc.vector.tensor_copy(picked[:, HALF:I], a_sb[:].indirect(half_of(l1, 1)))
         nc.scalar.activation(f1[:].indirect(l2[:]), picked[:], COPY)
 
-        b_tail = sb.tile([P, U - SPLIT], F32, name="b_tail")
-        nc.vector.tensor_copy(b_tail[:], b_banks[1][:, SPLIT - BANK:BANK])
+        b_head = sb.tile([P, U - SPLIT], F32, name="b_head")
+        share = U - SPLIT
+        nc.vector.tensor_copy(b_head[:], b_banks[0][:, 0:share])
         bb = sb.tile([P, U], F32, name="bb")
-        nc.vector.tensor_tensor(bb[:, 0:BANK], b_banks[0][:], f1[:, 0:BANK], ALU.add)
-        nc.vector.tensor_tensor(bb[:, BANK:SPLIT], b_banks[1][:, 0:SPLIT - BANK], f1[:, BANK:SPLIT], ALU.add)
-        nc.gpsimd.tensor_tensor(bb[:, SPLIT:U], b_tail[:], f1[:, SPLIT:U], ALU.add)
+        nc.gpsimd.tensor_tensor(bb[:, 0:share], b_head[:], f1[:, 0:share], ALU.add)
+        nc.vector.tensor_tensor(bb[:, share:BANK], b_banks[0][:, share:BANK], f1[:, share:BANK], ALU.add)
+        nc.vector.tensor_tensor(bb[:, BANK:U], b_banks[1][:], f1[:, BANK:U], ALU.add)
 
         g4 = []
         for h in range(2):
@@ -128,8 +133,9 @@ def tile_attend_doubleread_two_kernel(tc, query, cache_words, cache_scales, draf
             nc.scalar.activation(f2[:].indirect(half_of(l5, h)), w[:], COPY)
 
         aa = sb.tile([P, T], F32, name="aa")
-        nc.vector.tensor_tensor(aa[:, 0:BANK], a_banks[0][:], f2[:, 0:BANK], ALU.subtract)
-        nc.vector.tensor_tensor(aa[:, BANK:SPLIT], a_banks[1][:, 0:SPLIT - BANK], f2[:, BANK:SPLIT], ALU.subtract)
+        for n, (c0, c1) in enumerate(A_PIECES[:3]):
+            c1 = min(c1, SPLIT)
+            nc.vector.tensor_tensor(aa[:, c0:c1], a_banks[n][:, 0:c1 - c0], f2[:, c0:c1], ALU.subtract)
         nc.gpsimd.tensor_tensor(aa[:, SPLIT:T], a_sb[:, SPLIT:T], f2[:, SPLIT:T], ALU.subtract)
 
         y0 = sb.tile([P, HALF], F32, name="y0")

@@ -20,7 +20,7 @@ P = 128
 PACK = 4
 BANK = 512
 HALF = I // 2
-SPLIT = 704
+SPLIT = 680
 CHUNK = T // 4
 A_PIECES = ((0, 256), (256, 512), (512, 768), (768, 896), (896, 1024))
 
@@ -55,10 +55,6 @@ def tile_attend_doubleread_two_kernel(tc, query, cache_words, cache_scales, draf
 
         q_raw = sb.tile([P, PACK, Q], F32, name="q_raw")
         nc.sync.dma_start(q_raw[:], query.rearrange("(p j) q -> p j q", j=PACK))
-        for quad, queue in enumerate((nc.scalar, nc.sync, nc.scalar, nc.sync)):
-            rows = cache_scales[0, 4 * quad:4 * quad + 4, :].bitcast(I32)
-            queue.dma_start(cache_plane[32 * quad:32 * quad + 16, :].bitcast(I32),
-                            rows.rearrange("r (j c) -> j r c", j=4))
         cache_bytes = cache_words[0].rearrange("p n t -> p (n t)")
         cache_codes = []
         for h in range(2):
@@ -66,6 +62,11 @@ def tile_attend_doubleread_two_kernel(tc, query, cache_words, cache_scales, draf
             nc.sync.dma_start(codes[:].bitcast(I32),
                               cache_bytes[:, h * BANK * PACK:(h + 1) * BANK * PACK].bitcast(I32))
             cache_codes.append(codes)
+            if h == 0:
+                for quad in range(4):
+                    rows = cache_scales[0, 4 * quad:4 * quad + 4, :].bitcast(I32)
+                    nc.sync.dma_start(cache_plane[32 * quad:32 * quad + 16, :].bitcast(I32),
+                                      rows.rearrange("r (j c) -> j r c", j=4))
         l1 = load_list(offs, "l1")
         l2 = load_list(offs2, "l2")
         draft_codes = sb.tile([P, 2 * U], U8, name="draft_codes", align_bytes=64)

from contextlib import ExitStack

import concourse.mybir as mybir

D, T, U, I, Q = 512, 1024, 1024, 512, 128
FLOPS = 2 * D * Q * (T + U)

F32 = mybir.dt.float32
BF16 = mybir.dt.bfloat16
I32 = mybir.dt.int32
U32 = mybir.dt.uint32
U16 = mybir.dt.uint16
U8 = mybir.dt.uint8
FP8X4 = mybir.dt.float8_e4m3fn_x4
FP4X4 = mybir.dt.float4_e2m1fn_x4
COPY = mybir.ActivationFunctionType.Copy
ALU = mybir.AluOpType

P = 128
PACK = 4
BANK = 512
HALF = I // 2
SPLIT = 680
CHUNK = T // 4
A_PIECES = ((0, 256), (256, 512), (512, 768), (768, 896), (896, 1024))


def tile_attend_doubleread_two_kernel(tc, query, cache_words, cache_scales, draft_words, draft_scales,
                                       offs, offs2, offs3, offs4, offs5, offs6, out):
    nc = tc.nc
    with ExitStack() as ctx:
        lists = ctx.enter_context(tc.tile_pool(name="lists", bufs=1))
        sb = ctx.enter_context(tc.tile_pool(name="sb", bufs=1))
        psum = ctx.enter_context(tc.psum_pool(name="psum", bufs=1))

        def load_list(src, name):
            tile = lists.tile([P, I // 16], U16, name=name)
            nc.sync.dma_start(tile[:], src)
            return tile

        def half_of(tile, h):
            return tile[:, h * (HALF // 16):(h + 1) * (HALF // 16)]

        def load_scale_rows(plane, scales, queues):
            for quad in range(4):
                queues[quad].dma_start(plane[32 * quad:32 * quad + 4, :].bitcast(I32),
                                       scales[0, 4 * quad:4 * quad + 4, :].bitcast(I32))

        cache_plane = sb.tile([P, CHUNK], U8, name="cache_plane", align_bytes=64)
        draft_plane = sb.tile([P, U], U8, name="draft_plane", align_bytes=64)
        f1 = sb.tile([P, U], F32, name="f1")
        f2 = sb.tile([P, T], F32, name="f2")
        nc.vector.memset(f1[:], 0.0)
        nc.vector.memset(f2[:], 0.0)

        q_raw = sb.tile([P, PACK, Q], F32, name="q_raw")
        nc.sync.dma_start(q_raw[:], query.rearrange("(p j) q -> p j q", j=PACK))
        cache_bytes = cache_words[0].rearrange("p n t -> p (n t)")
        cache_codes = []
        for h in range(2):
            codes = sb.tile([P, BANK], U32, name="cache_codes%d" % h, align_bytes=64)
            nc.sync.dma_start(codes[:].bitcast(I32),
                              cache_bytes[:, h * BANK * PACK:(h + 1) * BANK * PACK].bitcast(I32))
            cache_codes.append(codes)
            if h == 0:
                for quad in range(4):
                    rows = cache_scales[0, 4 * quad:4 * quad + 4, :].bitcast(I32)
                    nc.sync.dma_start(cache_plane[32 * quad:32 * quad + 16, :].bitcast(I32),
                                      rows.rearrange("r (j c) -> j r c", j=4))
        l1 = load_list(offs, "l1")
        l2 = load_list(offs2, "l2")
        draft_codes = sb.tile([P, 2 * U], U8, name="draft_codes", align_bytes=64)
        nc.sync.dma_start(draft_codes[:].bitcast(I32), draft_words[0].bitcast(I32))
        load_scale_rows(draft_plane, draft_scales, (nc.sync,) * 4)
        l3 = load_list(offs3, "l3")
        l4 = load_list(offs4, "l4")
        l5 = load_list(offs5, "l5")
        l6 = load_list(offs6, "l6")

        q_bf = sb.tile([P, Q, PACK], BF16, name="q_bf", align_bytes=64)
        q_view = q_raw[:].rearrange("p j q -> p q j")
        nc.scalar.activation(q_bf[:, 0:Q // 2, :], q_view[:, 0:Q // 2, :], COPY)
        nc.vector.tensor_copy(q_bf[:, Q // 2:Q, :], q_view[:, Q // 2:Q, :])
        q_codes = sb.tile([P, Q], U32, name="q_codes", align_bytes=64)
        q_plane = sb.tile([P, Q], U8, name="q_plane", align_bytes=64)
        nc.vector.quantize_mx(q_codes[:].bitcast(FP8X4), q_plane[:], q_bf[:].rearrange("p q j -> p (q j)"))

        a_sb = sb.tile([P, T], F32, name="a_sb")
        a_banks = []
        for n, (c0, c1) in enumerate(A_PIECES):
            bank = psum.tile([P, BANK], F32, name="a_bank%d" % n, tag="bank%d" % n)
            h = c0 // BANK
            nc.tensor.matmul_mx(bank[:, 0:c1 - c0], lhsT=q_codes[:].bitcast(FP8X4), lhsT_scale=q_plane[:],
                                rhs=cache_codes[h][:, c0 - h * BANK:c1 - h * BANK].bitcast(FP8X4),
                                rhs_scale=cache_plane[4 * (c0 // CHUNK):P, c0 % CHUNK:c0 % CHUNK + c1 - c0], start=True, stop=True)
            a_banks.append(bank)
        for n, (c0, c1) in enumerate(A_PIECES):
            if n % 2 == 0:
                nc.scalar.copy(a_sb[:, c0:c1], a_banks[n][:, 0:c1 - c0])
            else:
                nc.vector.tensor_copy(a_sb[:, c0:c1], a_banks[n][:, 0:c1 - c0])

        b_banks = []
        for h in range(2):
            bank = psum.tile([P, BANK], F32, name="b_bank%d" % h, tag="bank%d" % (3 + h))
            nc.tensor.matmul_mx(bank[:], lhsT=q_codes[:].bitcast(FP8X4), lhsT_scale=q_plane[:],
                                rhs=draft_codes[:, 2 * h * BANK:2 * (h + 1) * BANK].bitcast(FP4X4),
                                rhs_scale=draft_plane[:, h * BANK:(h + 1) * BANK], start=True, stop=True)
            b_banks.append(bank)

        picked = sb.tile([P, I], F32, name="picked")
        nc.scalar.activation(picked[:, 0:HALF], a_sb[:].indirect(half_of(l1, 0)), COPY)
        nc.vector.tensor_copy(picked[:, HALF:I], a_sb[:].indirect(half_of(l1, 1)))
        nc.scalar.activation(f1[:].indirect(l2[:]), picked[:], COPY)

        b_head = sb.tile([P, U - SPLIT], F32, name="b_head")
        share = U - SPLIT
        nc.vector.tensor_copy(b_head[:], b_banks[0][:, 0:share])
        bb = sb.tile([P, U], F32, name="bb")
        nc.gpsimd.tensor_tensor(bb[:, 0:share], b_head[:], f1[:, 0:share], ALU.add)
        nc.vector.tensor_tensor(bb[:, share:BANK], b_banks[0][:, share:BANK], f1[:, share:BANK], ALU.add)
        nc.vector.tensor_tensor(bb[:, BANK:U], b_banks[1][:], f1[:, BANK:U], ALU.add)

        g4 = []
        for h in range(2):
            g = sb.tile([P, HALF], F32, name="g4_%d" % h)
            nc.scalar.activation(g[:], bb[:].indirect(half_of(l4, h)), COPY)
            g4.append(g)
        for h in range(2):
            g3 = sb.tile([P, HALF], F32, name="g3")
            w = sb.tile([P, HALF], F32, name="w%d" % h)
            nc.vector.tensor_copy(g3[:], bb[:].indirect(half_of(l3, h)))
            nc.vector.tensor_tensor(w[:], g3[:], g4[h][:], ALU.max)
            nc.scalar.activation(f2[:].indirect(half_of(l5, h)), w[:], COPY)

        aa = sb.tile([P, T], F32, name="aa")
        for n, (c0, c1) in enumerate(A_PIECES[:3]):
            c1 = min(c1, SPLIT)
            nc.vector.tensor_tensor(aa[:, c0:c1], a_banks[n][:, 0:c1 - c0], f2[:, c0:c1], ALU.subtract)
        nc.gpsimd.tensor_tensor(aa[:, SPLIT:T], a_sb[:, SPLIT:T], f2[:, SPLIT:T], ALU.subtract)

        y0 = sb.tile([P, HALF], F32, name="y0")
        y1 = sb.tile([P, HALF], F32, name="y1")
        nc.vector.tensor_copy(y0[:], aa[:].indirect(half_of(l6, 0)))
        nc.scalar.activation(y1[:], aa[:].indirect(half_of(l6, 1)), COPY)
        nc.sync.dma_start(out[:, 0:HALF], y0[:])
        nc.scalar.dma_start(out[:, HALF:I], y1[:])
